import numpy as np, ml_dtypes
CORES = [73,201,329,457,330]
N = 5
KT, C = 1, 128
def setup_inputs(rng):
    return {"x": rng.standard_normal((N, 128, KT * C), dtype=np.float32).astype(ml_dtypes.bfloat16)}
def setup_inputs_big(rng):
    d = setup_inputs(rng)
    for k in ("x",): d[k] = (d[k].astype(np.float32) * 1024.0).astype(d[k].dtype)
    return d
def setup_inputs_small(rng):
    d = setup_inputs(rng)
    for k in ("x",): d[k] = (d[k].astype(np.float32) * (1 / 1024.0)).astype(d[k].dtype)
    return d
def setup_inputs_apart(rng):
    d = setup_inputs(rng)
    f = (10.0 ** rng.permutation(np.linspace(-1.5, 1.5, N))).astype(np.float32).reshape(N, 1, 1)
    for k in ("x",): d[k] = (d[k].astype(np.float32) * f).astype(d[k].dtype)
    return d
def reference(x):
    X = x.astype(np.float64)
    y = np.full((N, C, N * C), np.nan)
    for r in range(N):
        for i in range(N):
            s = i
            if s != r: y[r][:, C * i:C * i + C] = sum(X[r][:, C * t:C * t + C].T @ X[s][:, C * t:C * t + C] for t in range(KT))
    return {"y": y.astype(ml_dtypes.bfloat16 if x.dtype != np.float64 else np.float64)}

@@ -1,0 +1,136 @@
+from concourse.bass import DstId, RemoteDMATransfer
+
+N = 5
+C = 128
+
+SCRATCH = {
+    "xd": ("dram", [C, C], "bfloat16"),
+    "ld": ("dram", [N, C, C], "bfloat16"),
+    "xs": ("sbuf", [C, N * C], "bfloat16"),
+    "ob": ("sbuf", [C, N * C], "bfloat16"),
+    "p0": ("psum", [C, 512], "float32"),
+    "p1": ("psum", [C, 512], "float32"),
+    "p2": ("psum", [C, 512], "float32"),
+    "pl": ("psum", [C, 512], "float32"),
+}
+SEMAPHORES = (["ldd", "lds", "ls", "st", "ml", "vl"] + ["a%d" % s for s in range(N)] + ["c%d" % s for s in range(N)]
+              + ["m%d" % s for s in range(N)] + ["v%d" % s for s in range(N)])
+
+
+def _plan(cores, topo):
+    R = range(len(cores))
+
+    def ok(a, b):
+        return a != b and topo.may_write(cores[a], cores[b])
+
+    far = [(s, d) for s in R for d in R if s != d and not ok(s, d)]
+    late_in = [sum(1 for _, d in far if d == m) for m in R]
+    load = [0 for _ in R]
+    relay = {}
+    for s, d in far:
+        m = min((m for m in R if ok(s, m) and ok(m, d)), key=lambda m: (load[m], late_in[m], -m))
+        relay[(s, d)] = m
+        load[m] += 1
+    calls = []
+    for r in R:
+        near = [d for d in R if ok(r, d)]
+        fw = [(s, d) for (s, d) in far if relay[(s, d)] == r]
+        pool = topo.mask(cores[r], cores[near[0]])
+        for d in near:
+            pool &= topo.mask(cores[r], cores[d])
+        eng = [e for e in range(pool.bit_length()) if (pool >> e) & 1]
+        crit = [d for d in near if any(s == r and relay[(s, t)] == d for s, t in far)]
+        rest = [d for d in near if d not in crit]
+        first, second = eng[0::2], eng[1::2]
+        mine = [[(r, [d], first[i::len(crit)], "dram") for i, d in enumerate(crit)]]
+        if rest:
+            mine.append([(r, rest, second, "dram")])
+        if fw:
+            mine.append([(s, [d], eng[i::len(fw)], "sbuf") for i, (s, d) in enumerate(fw)])
+        calls.append(mine)
+    return calls
+
+
+def rank_program(g, core, T, topo):
+    r = T.rank_of(core)
+    if r is None:
+        return
+    cores = T.cores
+    sem = T.sem
+    calls = _plan(cores, topo)
+
+    def blk(t, lo, hi=None):
+        return t[:, lo * C:((lo if hi is None else hi) + 1) * C]
+
+    inc = {}
+    for q in range(len(cores)):
+        for k, call in enumerate(calls[q]):
+            for s, dsts, engs, where in call:
+                if r in dsts:
+                    inc[s] = (len(engs), where, k)
+    early = sorted((s for s in inc if inc[s][1] == "dram"), key=lambda s: (inc[s][2], s))
+    late = sorted(s for s in inc if inc[s][1] == "sbuf")
+    lo, hi = min(late), max(late)
+    head = [s for s in early if not lo <= s <= hi]
+
+    g.sync.dma_start(T.xd[:], T.x[:]).then_inc(sem.ldd, 16)
+    g.scalar.dma_start(blk(T.xs, r), T.x[:]).then_inc(sem.lds, 16)
+
+    g.wait_ge(sem.ldd, 16)
+    left = 0
+    for call in calls[r]:
+        trs = []
+        for s, dsts, engs, where in call:
+            if s != r:
+                g.wait_ge(sem["a%d" % s], inc[s][0])
+            ids = []
+            for d in dsts:
+                rid, pid = topo.addr(cores[d], core)
+                ids.append(DstId(rid=rid, pnc=pid))
+            dst = T.ld[s] if where == "dram" else blk(T.xs, s)
+            trs.append(RemoteDMATransfer(dst_ids=ids, dma_engine_mask=sum(1 << e for e in engs),
+                                         remote_sem=sem["a%d" % s], srcs=[T.xd[:] if s == r else T.ld[s]],
+                                         dsts=[dst for _ in dsts], alu_op=0))
+            left += len(engs)
+        g.remote_dma_fused(trs, local_sem=sem.ls)
+
+    dq = (g.sync, g.scalar)
+    for i, s in enumerate(early):
+        dq[i % 2].wait_ge(sem["a%d" % s], inc[s][0])
+        dq[i % 2].dma_start(blk(T.xs, s), T.ld[s]).then_inc(sem["c%d" % s], 16)
+
+    own = blk(T.xs, r)
+    g.tensor.wait_ge(sem.lds, 16)
+    for i, s in enumerate(head):
+        g.tensor.wait_ge(sem["c%d" % s], 16)
+        g.tensor.matmul(T["p%d" % i][:, 0:C], own, blk(T.xs, s), True, True).then_inc(sem["m%d" % s], 1)
+    for s in range(lo, hi + 1):
+        if s in late:
+            g.tensor.wait_ge(sem["a%d" % s], inc[s][0])
+        elif s != r:
+            g.tensor.wait_ge(sem["c%d" % s], 16)
+    w = (hi - lo + 1) * C
+    g.tensor.matmul(T.pl[:, 0:w], own, blk(T.xs, lo, hi), True, True).then_inc(sem.ml, 1)
+
+    for i, s in enumerate(head):
+        g.vector.wait_ge(sem["m%d" % s], 1)
+        g.vector.tensor_copy(blk(T.ob, s), T["p%d" % i][:, 0:C]).then_inc(sem["v%d" % s], 1)
+    g.vector.wait_ge(sem.ml, 1)
+    g.vector.tensor_copy(blk(T.ob, lo, hi), T.pl[:, 0:w]).then_inc(sem.vl, 1)
+
+    runs = []
+    for s in sorted(head):
+        if runs and runs[-1][-1] == s - 1:
+            runs[-1].append(s)
+        else:
+            runs.append([s])
+    runs.sort(key=lambda run: max(head.index(s) for s in run))
+    for run in runs:
+        for s in run:
+            g.sync.wait_ge(sem["v%d" % s], 1)
+        g.sync.dma_start(blk(T.y, run[0], run[-1]), blk(T.ob, run[0], run[-1])).then_inc(sem.st, 16)
+    g.scalar.wait_ge(sem.vl, 1)
+    g.scalar.dma_start(blk(T.y, lo, hi), blk(T.ob, lo, hi)).then_inc(sem.st, 16)
+
+    g.wait_ge(sem.ls, left)
+    g.wait_ge(sem.st, 16 * (len(runs) + 1))

@@ -1,4 +1,5 @@
 from concourse.bass import DstId, RemoteDMATransfer
+from concourse.mybir import ActivationFunctionType
 
 N = 5
 C = 128
@@ -11,9 +12,9 @@ SCRATCH = {
     "p0": ("psum", [C, 512], "float32"),
     "p1": ("psum", [C, 512], "float32"),
     "p2": ("psum", [C, 512], "float32"),
-    "pl": ("psum", [C, 512], "float32"),
+    "p3": ("psum", [C, 512], "float32"),
 }
-SEMAPHORES = (["ldd", "lds", "ls", "st", "ml", "vl"] + ["a%d" % s for s in range(N)] + ["c%d" % s for s in range(N)]
+SEMAPHORES = (["ldd", "lds", "ls", "st"] + ["a%d" % s for s in range(N)] + ["d%d" % s for s in range(N)]
               + ["m%d" % s for s in range(N)] + ["v%d" % s for s in range(N)])
 
 
@@ -23,32 +24,89 @@ def _plan(cores, topo):
     def ok(a, b):
         return a != b and topo.may_write(cores[a], cores[b])
 
+    def chipmate(a, b):
+        return a != b and (topo.host(cores[a]), topo.chip(cores[a])) == (topo.host(cores[b]), topo.chip(cores[b]))
+
     far = [(s, d) for s in R for d in R if s != d and not ok(s, d)]
     late_in = [sum(1 for _, d in far if d == m) for m in R]
     load = [0 for _ in R]
     relay = {}
     for s, d in far:
-        m = min((m for m in R if ok(s, m) and ok(m, d)), key=lambda m: (load[m], late_in[m], -m))
+        m = min((m for m in R if ok(s, m) and ok(m, d)),
+                key=lambda m: (not any(relay[p] == m and (p[0] == s or p[1] == d) for p in relay),
+                               load[m], late_in[m], -m))
         relay[(s, d)] = m
         load[m] += 1
+    hand = {}
+    for s in R:
+        for d in R:
+            if ok(s, d) and not chipmate(s, d):
+                for m in R:
+                    if chipmate(m, d) and any(p[0] == s and relay[p] == m for p in relay):
+                        hand[(s, d)] = m
+    order = []
+    for m in R:
+        for d in R:
+            ss = [s for s in R if relay.get((s, d)) == m]
+            if len(ss) > 1:
+                order += [s for s in ss if s not in order]
+    order += [s for s in R if s not in order]
+    pos = {s: i for i, s in enumerate(order)}
+
     calls = []
     for r in R:
-        near = [d for d in R if ok(r, d)]
-        fw = [(s, d) for (s, d) in far if relay[(s, d)] == r]
-        pool = topo.mask(cores[r], cores[near[0]])
-        for d in near:
+        near = [d for d in R if ok(r, d) and (r, d) not in hand]
+        off = [d for d in near if not chipmate(r, d)]
+        onc = [d for d in near if chipmate(r, d)]
+        pool = topo.mask(cores[r], cores[off[0]])
+        for d in off:
             pool &= topo.mask(cores[r], cores[d])
         eng = [e for e in range(pool.bit_length()) if (pool >> e) & 1]
-        crit = [d for d in near if any(s == r and relay[(s, t)] == d for s, t in far)]
-        rest = [d for d in near if d not in crit]
-        first, second = eng[0::2], eng[1::2]
-        mine = [[(r, [d], first[i::len(crit)], "dram") for i, d in enumerate(crit)]]
-        if rest:
-            mine.append([(r, rest, second, "dram")])
-        if fw:
-            mine.append([(s, [d], eng[i::len(fw)], "sbuf") for i, (s, d) in enumerate(fw)])
+        inner = []
+        for d in R:
+            if chipmate(r, d):
+                wide = topo.mask(cores[r], cores[d]) & ~pool
+                inner = [e for e in range(wide.bit_length()) if (wide >> e) & 1]
+        crit = [d for d in off if any(p[0] == r and relay[p] == d for p in relay)]
+        staged = [d for d in crit if sum(1 for p in relay if p[0] == r and relay[p] == d) > 1]
+        rest = [d for d in off if d not in crit]
+        mine = []
+        one = []
+        for i, d in enumerate(crit):
+            e = eng[i::len(crit)]
+            one.append(([r], [d], e[0::2], "own", "dram") if d in staged else ([r], [d], e, "own", "sbuf"))
+        mine.append(one)
+        two = []
+        if rest + staged:
+            two.append(([r], rest + staged, eng, "own", "sbuf"))
+        if onc:
+            two.append(([r], onc, inner, "own", "sbuf"))
+        if two:
+            mine.append(two)
+        fw = [p for p in far if relay[p] == r]
+        tr = []
+        done = []
+        for d in R:
+            ss = [s for s, t in fw if t == d]
+            if len(ss) > 1:
+                tr.append((sorted(ss, key=lambda s: pos[s]), [d]))
+                done += [(s, d) for s in ss]
+        for s in R:
+            dd = [t for q, t in fw if q == s and (q, t) not in done]
+            if dd:
+                tr.append(([s], dd))
+        for width in sorted({len(ss) for ss, _ in tr}):
+            same = [t for t in tr if len(t[0]) == width]
+            call = [(ss, dd, eng[i::len(same)], "ld" if len(dd) > 1 else "xs", "sbuf")
+                    for i, (ss, dd) in enumerate(same)]
+            if width == 1:
+                for s in R:
+                    dd = [d for d in R if hand.get((s, d)) == r]
+                    if dd:
+                        call.append(([s], dd, inner, "xs", "sbuf"))
+            mine.append(call)
         calls.append(mine)
-    return calls
+    return calls, pos
 
 
 def rank_program(g, core, T, topo):
@@ -57,80 +115,81 @@ def rank_program(g, core, T, topo):
         return
     cores = T.cores
     sem = T.sem
-    calls = _plan(cores, topo)
+    calls, pos = _plan(cores, topo)
 
-    def blk(t, lo, hi=None):
-        return t[:, lo * C:((lo if hi is None else hi) + 1) * C]
+    def xb(ss):
+        return T.xs[:, pos[ss[0]] * C:(pos[ss[-1]] + 1) * C]
 
-    inc = {}
+    def yb(t, lo, hi):
+        return t[:, lo * C:(hi + 1) * C]
+
+    arr, slot = {}, {}
     for q in range(len(cores)):
         for k, call in enumerate(calls[q]):
-            for s, dsts, engs, where in call:
+            for ss, dsts, engs, src, where in call:
                 if r in dsts:
-                    inc[s] = (len(engs), where, k)
-    early = sorted((s for s in inc if inc[s][1] == "dram"), key=lambda s: (inc[s][2], s))
-    late = sorted(s for s in inc if inc[s][1] == "sbuf")
-    lo, hi = min(late), max(late)
-    head = [s for s in early if not lo <= s <= hi]
+                    for s in ss:
+                        if where == "dram":
+                            slot[s] = (sem["d%d" % ss[0]], len(engs))
+                        else:
+                            arr[s] = (sem["a%d" % ss[0]], len(engs), 1 if src == "own" else 2, k)
+    early = sorted((s for s in arr if arr[s][2] == 1), key=lambda s: (arr[s][3], s))
+    late = sorted(s for s in arr if arr[s][2] == 2)
+    bank = {s: T["p%d" % i] for i, s in enumerate(early + late)}
 
     g.sync.dma_start(T.xd[:], T.x[:]).then_inc(sem.ldd, 16)
-    g.scalar.dma_start(blk(T.xs, r), T.x[:]).then_inc(sem.lds, 16)
+    g.scalar.dma_start(xb([r]), T.x[:]).then_inc(sem.lds, 16)
 
     g.wait_ge(sem.ldd, 16)
     left = 0
     for call in calls[r]:
         trs = []
-        for s, dsts, engs, where in call:
-            if s != r:
-                g.wait_ge(sem["a%d" % s], inc[s][0])
+        for ss, dsts, engs, src, where in call:
+            if src == "ld":
+                g.wait_ge(slot[ss[0]][0], slot[ss[0]][1])
+            elif src == "xs":
+                for s in ss:
+                    g.wait_ge(arr[s][0], arr[s][1])
             ids = []
             for d in dsts:
                 rid, pid = topo.addr(cores[d], core)
                 ids.append(DstId(rid=rid, pnc=pid))
-            dst = T.ld[s] if where == "dram" else blk(T.xs, s)
+            dst = T.ld[ss[0]] if where == "dram" else xb(ss)
+            frm = T.xd[:] if src == "own" else T.ld[ss[0]] if src == "ld" else xb(ss)
             trs.append(RemoteDMATransfer(dst_ids=ids, dma_engine_mask=sum(1 << e for e in engs),
-                                         remote_sem=sem["a%d" % s], srcs=[T.xd[:] if s == r else T.ld[s]],
+                                         remote_sem=sem[("d%d" if where == "dram" else "a%d") % ss[0]], srcs=[frm],
                                          dsts=[dst for _ in dsts], alu_op=0))
             left += len(engs)
         g.remote_dma_fused(trs, local_sem=sem.ls)
 
-    dq = (g.sync, g.scalar)
-    for i, s in enumerate(early):
-        dq[i % 2].wait_ge(sem["a%d" % s], inc[s][0])
-        dq[i % 2].dma_start(blk(T.xs, s), T.ld[s]).then_inc(sem["c%d" % s], 16)
-
-    own = blk(T.xs, r)
+    own = xb([r])
     g.tensor.wait_ge(sem.lds, 16)
-    for i, s in enumerate(head):
-        g.tensor.wait_ge(sem["c%d" % s], 16)
-        g.tensor.matmul(T["p%d" % i][:, 0:C], own, blk(T.xs, s), True, True).then_inc(sem["m%d" % s], 1)
-    for s in range(lo, hi + 1):
-        if s in late:
-            g.tensor.wait_ge(sem["a%d" % s], inc[s][0])
-        elif s != r:
-            g.tensor.wait_ge(sem["c%d" % s], 16)
-    w = (hi - lo + 1) * C
-    g.tensor.matmul(T.pl[:, 0:w], own, blk(T.xs, lo, hi), True, True).then_inc(sem.ml, 1)
+    for s in early + late:
+        g.tensor.wait_ge(arr[s][0], arr[s][1])
+        g.tensor.matmul(bank[s][:, 0:C], own, xb([s]), True, True).then_inc(sem["m%d" % s], 1)
 
-    for i, s in enumerate(head):
+    for s in early + late[0::2]:
         g.vector.wait_ge(sem["m%d" % s], 1)
-        g.vector.tensor_copy(blk(T.ob, s), T["p%d" % i][:, 0:C]).then_inc(sem["v%d" % s], 1)
-    g.vector.wait_ge(sem.ml, 1)
-    g.vector.tensor_copy(blk(T.ob, lo, hi), T.pl[:, 0:w]).then_inc(sem.vl, 1)
+        g.vector.tensor_copy(yb(T.ob, s, s), bank[s][:, 0:C]).then_inc(sem["v%d" % s], 1)
 
     runs = []
-    for s in sorted(head):
+    for s in sorted(early):
         if runs and runs[-1][-1] == s - 1:
             runs[-1].append(s)
         else:
             runs.append([s])
-    runs.sort(key=lambda run: max(head.index(s) for s in run))
-    for run in runs:
+    runs.sort(key=lambda run: max(early.index(s) for s in run))
+    dq = (g.sync, g.scalar)
+    for i, run in enumerate(runs):
         for s in run:
-            g.sync.wait_ge(sem["v%d" % s], 1)
-        g.sync.dma_start(blk(T.y, run[0], run[-1]), blk(T.ob, run[0], run[-1])).then_inc(sem.st, 16)
-    g.scalar.wait_ge(sem.vl, 1)
-    g.scalar.dma_start(blk(T.y, lo, hi), blk(T.ob, lo, hi)).then_inc(sem.st, 16)
+            dq[i % 2].wait_ge(sem["v%d" % s], 1)
+        dq[i % 2].dma_start(yb(T.y, run[0], run[-1]), yb(T.ob, run[0], run[-1])).then_inc(sem.st, 16)
+    for s in late[1::2]:
+        g.scalar.wait_ge(sem["m%d" % s], 1)
+        g.scalar.activation(yb(T.ob, s, s), bank[s][:, 0:C], ActivationFunctionType.Copy).then_inc(sem["v%d" % s], 1)
+    for i, s in enumerate(late):
+        dq[i % 2].wait_ge(sem["v%d" % s], 1)
+        dq[i % 2].dma_start(yb(T.y, s, s), yb(T.ob, s, s)).then_inc(sem.st, 16)
 
     g.wait_ge(sem.ls, left)
-    g.wait_ge(sem.st, 16 * (len(runs) + 1))
+    g.wait_ge(sem.st, 16 * (len(runs) + len(late)))

from concourse.bass import DstId, RemoteDMATransfer
from concourse.mybir import ActivationFunctionType

N = 5
C = 128

SCRATCH = {
    "xd": ("dram", [C, C], "bfloat16"),
    "ld": ("dram", [N, C, C], "bfloat16"),
    "xs": ("sbuf", [C, N * C], "bfloat16"),
    "ob": ("sbuf", [C, N * C], "bfloat16"),
    "p0": ("psum", [C, 512], "float32"),
    "p1": ("psum", [C, 512], "float32"),
    "p2": ("psum", [C, 512], "float32"),
    "p3": ("psum", [C, 512], "float32"),
}
SEMAPHORES = (["ldd", "lds", "ls", "st"] + ["a%d" % s for s in range(N)] + ["d%d" % s for s in range(N)]
              + ["m%d" % s for s in range(N)] + ["v%d" % s for s in range(N)])


def _plan(cores, topo):
    R = range(len(cores))

    def ok(a, b):
        return a != b and topo.may_write(cores[a], cores[b])

    def chipmate(a, b):
        return a != b and (topo.host(cores[a]), topo.chip(cores[a])) == (topo.host(cores[b]), topo.chip(cores[b]))

    far = [(s, d) for s in R for d in R if s != d and not ok(s, d)]
    late_in = [sum(1 for _, d in far if d == m) for m in R]
    load = [0 for _ in R]
    relay = {}
    for s, d in far:
        m = min((m for m in R if ok(s, m) and ok(m, d)),
                key=lambda m: (not any(relay[p] == m and (p[0] == s or p[1] == d) for p in relay),
                               load[m], late_in[m], -m))
        relay[(s, d)] = m
        load[m] += 1
    hand = {}
    for s in R:
        for d in R:
            if ok(s, d) and not chipmate(s, d):
                for m in R:
                    if chipmate(m, d) and any(p[0] == s and relay[p] == m for p in relay):
                        hand[(s, d)] = m
    order = []
    for m in R:
        for d in R:
            ss = [s for s in R if relay.get((s, d)) == m]
            if len(ss) > 1:
                order += [s for s in ss if s not in order]
    order += [s for s in R if s not in order]
    pos = {s: i for i, s in enumerate(order)}

    calls = []
    for r in R:
        near = [d for d in R if ok(r, d) and (r, d) not in hand]
        off = [d for d in near if not chipmate(r, d)]
        onc = [d for d in near if chipmate(r, d)]
        pool = topo.mask(cores[r], cores[off[0]])
        for d in off:
            pool &= topo.mask(cores[r], cores[d])
        eng = [e for e in range(pool.bit_length()) if (pool >> e) & 1]
        inner = []
        for d in R:
            if chipmate(r, d):
                wide = topo.mask(cores[r], cores[d]) & ~pool
                inner = [e for e in range(wide.bit_length()) if (wide >> e) & 1]
        crit = [d for d in off if any(p[0] == r and relay[p] == d for p in relay)]
        staged = [d for d in crit if sum(1 for p in relay if p[0] == r and relay[p] == d) > 1]
        rest = [d for d in off if d not in crit]
        mine = []
        one = []
        for i, d in enumerate(crit):
            e = eng[i::len(crit)]
            one.append(([r], [d], e[0::2], "own", "dram") if d in staged else ([r], [d], e, "own", "sbuf"))
        mine.append(one)
        two = []
        if rest + staged:
            two.append(([r], rest + staged, eng, "own", "sbuf"))
        if onc:
            two.append(([r], onc, inner, "own", "sbuf"))
        if two:
            mine.append(two)
        fw = [p for p in far if relay[p] == r]
        tr = []
        done = []
        for d in R:
            ss = [s for s, t in fw if t == d]
            if len(ss) > 1:
                tr.append((sorted(ss, key=lambda s: pos[s]), [d]))
                done += [(s, d) for s in ss]
        for s in R:
            dd = [t for q, t in fw if q == s and (q, t) not in done]
            if dd:
                tr.append(([s], dd))
        for width in sorted({len(ss) for ss, _ in tr}):
            same = [t for t in tr if len(t[0]) == width]
            call = [(ss, dd, eng[i::len(same)], "ld" if len(dd) > 1 else "xs", "sbuf")
                    for i, (ss, dd) in enumerate(same)]
            if width == 1:
                for s in R:
                    dd = [d for d in R if hand.get((s, d)) == r]
                    if dd:
                        call.append(([s], dd, inner, "xs", "sbuf"))
            mine.append(call)
        calls.append(mine)
    return calls, pos


def rank_program(g, core, T, topo):
    r = T.rank_of(core)
    if r is None:
        return
    cores = T.cores
    sem = T.sem
    calls, pos = _plan(cores, topo)

    def xb(ss):
        return T.xs[:, pos[ss[0]] * C:(pos[ss[-1]] + 1) * C]

    def yb(t, lo, hi):
        return t[:, lo * C:(hi + 1) * C]

    arr, slot = {}, {}
    for q in range(len(cores)):
        for k, call in enumerate(calls[q]):
            for ss, dsts, engs, src, where in call:
                if r in dsts:
                    for s in ss:
                        if where == "dram":
                            slot[s] = (sem["d%d" % ss[0]], len(engs))
                        else:
                            arr[s] = (sem["a%d" % ss[0]], len(engs), 1 if src == "own" else 2, k)
    early = sorted((s for s in arr if arr[s][2] == 1), key=lambda s: (arr[s][3], s))
    late = sorted(s for s in arr if arr[s][2] == 2)
    bank = {s: T["p%d" % i] for i, s in enumerate(early + late)}

    g.sync.dma_start(T.xd[:], T.x[:]).then_inc(sem.ldd, 16)
    g.scalar.dma_start(xb([r]), T.x[:]).then_inc(sem.lds, 16)

    g.wait_ge(sem.ldd, 16)
    left = 0
    for call in calls[r]:
        trs = []
        for ss, dsts, engs, src, where in call:
            if src == "ld":
                g.wait_ge(slot[ss[0]][0], slot[ss[0]][1])
            elif src == "xs":
                for s in ss:
                    g.wait_ge(arr[s][0], arr[s][1])
            ids = []
            for d in dsts:
                rid, pid = topo.addr(cores[d], core)
                ids.append(DstId(rid=rid, pnc=pid))
            dst = T.ld[ss[0]] if where == "dram" else xb(ss)
            frm = T.xd[:] if src == "own" else T.ld[ss[0]] if src == "ld" else xb(ss)
            trs.append(RemoteDMATransfer(dst_ids=ids, dma_engine_mask=sum(1 << e for e in engs),
                                         remote_sem=sem[("d%d" if where == "dram" else "a%d") % ss[0]], srcs=[frm],
                                         dsts=[dst for _ in dsts], alu_op=0))
            left += len(engs)
        g.remote_dma_fused(trs, local_sem=sem.ls)

    own = xb([r])
    g.tensor.wait_ge(sem.lds, 16)
    for s in early + late:
        g.tensor.wait_ge(arr[s][0], arr[s][1])
        g.tensor.matmul(bank[s][:, 0:C], own, xb([s]), True, True).then_inc(sem["m%d" % s], 1)

    for s in early + late[0::2]:
        g.vector.wait_ge(sem["m%d" % s], 1)
        g.vector.tensor_copy(yb(T.ob, s, s), bank[s][:, 0:C]).then_inc(sem["v%d" % s], 1)

    runs = []
    for s in sorted(early):
        if runs and runs[-1][-1] == s - 1:
            runs[-1].append(s)
        else:
            runs.append([s])
    runs.sort(key=lambda run: max(early.index(s) for s in run))
    dq = (g.sync, g.scalar)
    for i, run in enumerate(runs):
        for s in run:
            dq[i % 2].wait_ge(sem["v%d" % s], 1)
        dq[i % 2].dma_start(yb(T.y, run[0], run[-1]), yb(T.ob, run[0], run[-1])).then_inc(sem.st, 16)
    for s in late[1::2]:
        g.scalar.wait_ge(sem["m%d" % s], 1)
        g.scalar.activation(yb(T.ob, s, s), bank[s][:, 0:C], ActivationFunctionType.Copy).then_inc(sem["v%d" % s], 1)
    for i, s in enumerate(late):
        dq[i % 2].wait_ge(sem["v%d" % s], 1)
        dq[i % 2].dma_start(yb(T.y, s, s), yb(T.ob, s, s)).then_inc(sem.st, 16)

    g.wait_ge(sem.ls, left)
    g.wait_ge(sem.st, 16 * (len(runs) + len(late)))
